import numpy as np
import ml_dtypes


def mxq(x, axis, fmt="e4m3"):
    dtype, down = {"e4m3": (ml_dtypes.float8_e4m3fn, 7), "e5m2": (ml_dtypes.float8_e5m2, 14)}[fmt]
    v = np.moveaxis(np.asarray(x, np.float32).astype(ml_dtypes.bfloat16).astype(np.float64), axis, -1)
    blocks = v.reshape(v.shape[:-1] + (-1, 32))
    amax = np.abs(blocks).max(-1, keepdims=True)
    byte = np.maximum(np.where(amax > 0, np.frexp(amax)[1] - 1 + 127, 0) - down, 1)
    scale = np.exp2(byte - 127.0)
    codes = (blocks / scale).astype(np.float32).astype(dtype).astype(np.float64)
    return np.moveaxis((codes * scale).reshape(v.shape), -1, axis)


WIDE = False


def mx_kscale(k):
    if not WIDE:
        return np.ones(k)
    levels = np.array([10, -10, 5, -5, 0])
    if k % 512:
        return np.exp2(np.random.permutation(np.resize(levels, k // 32))).repeat(32)
    a = np.empty((k // 512, 16))
    for p in range(k // 512):
        a[p, :8] = np.random.permutation(np.resize(levels, 8))
        for g in range(8):
            far = levels[np.abs(levels - a[p, g]) >= 10]
            a[p, g + 8] = far[np.random.randint(len(far))]
    return np.exp2(a.ravel()).repeat(32)


def f64(x):
    return np.asarray(x).astype(np.float64)


def striped8(idx):
    return np.asarray(idx).reshape(8, -1, 16).transpose(0, 2, 1).reshape(128, -1).astype(np.uint16)


def unstriped8(offs):
    return offs.reshape(8, 16, -1).transpose(0, 2, 1).reshape(8, -1).astype(np.int64)


def pick8(x, idx, run):
    r = np.arange(len(x))
    return x[r[:, None], idx[r % (8 * run) // run]]


E2M1 = np.array([0.0, 0.5, 1.0, 1.5, 2.0, 3.0, 4.0, 6.0, -0.0, -0.5, -1.0, -1.5, -2.0, -3.0, -4.0, -6.0])


def pack_weight(w, fmt):
    k, n = w.shape
    w = f64(np.asarray(w, np.float32).astype(ml_dtypes.bfloat16)).reshape(k // 32, 32, n)
    amax = np.abs(w).max(1)
    if fmt == "e4m3":
        byte = np.frexp(amax)[1] - 1 + 127 - 7
    else:
        mant, ex = np.frexp(amax / 6.0)
        byte = np.where(mant > 0.5, ex, ex - 1) + 127
    byte = np.clip(np.where(amax > 0, byte, 1), 1, 254)
    scaled = (w * np.exp2(127.0 - byte)[:, None, :]).reshape(k, n).astype(np.float32)
    by_word = np.ascontiguousarray(scaled.reshape(k // 512, 128, 4, n).transpose(0, 1, 3, 2))
    if fmt == "e4m3":
        words = by_word.astype(ml_dtypes.float8_e4m3fn).view(np.uint8)
    else:
        c = by_word.astype(ml_dtypes.float4_e2m1fn).view(np.uint8) & 0xF
        words = (c[..., 0::2] | (c[..., 1::2] << 4)).reshape(k // 512, 128, 2 * n)
    return np.ascontiguousarray(words), np.ascontiguousarray(byte.astype(np.uint8).reshape(k // 512, 16, n))


def unpack_weight(words, scales, fmt):
    g, _, n = scales.shape
    words = np.ascontiguousarray(words).reshape(g, 128, n, -1)
    if fmt == "e4m3":
        vals = words.view(ml_dtypes.float8_e4m3fn).astype(np.float64)
    else:
        nib = np.empty((g, 128, n, 4), np.uint8)
        nib[..., 0::2] = words & 0xF
        nib[..., 1::2] = words >> 4
        vals = E2M1[nib]
    vals = vals * np.repeat(np.exp2(scales.astype(np.float64) - 127.0), 8, axis=1)[..., None]
    return vals.transpose(0, 1, 3, 2).reshape(g * 512, n)


D, T, U, X, S, I, Q = 512, 1024, 1024, 1024, 1024, 512, 128


def setup_inputs():
    n = np.random.standard_normal
    idx = np.stack([np.random.permutation(T)[:I] for _ in range(8)])
    idx2 = np.stack([np.random.permutation(U)[:I] for _ in range(8)])
    idx3 = np.stack([np.random.permutation(X)[:I] for _ in range(8)])
    idx4 = np.stack([np.random.permutation(S)[:I] for _ in range(8)])
    idx5 = np.stack([np.random.permutation(X)[:I] for _ in range(8)])
    fd = mx_kscale(D)
    keysp = pack_weight(n((D, T)) / fd[:, None], "e2m1")
    notesp = pack_weight(n((D, U)) / fd[:, None], "e4m3")
    usersp = pack_weight(n((D, X)) / fd[:, None], "e2m1")
    shelvesp = pack_weight(n((D, S)) / fd[:, None], "e4m3")
    return {
        "query": (n((D, Q)) * 1.0 / np.sqrt(D) * fd[:, None]).astype(np.float32),
        "keys_words": keysp[0],
        "keys_scales": keysp[1],
        "notes_words": notesp[0],
        "notes_scales": notesp[1],
        "users_words": usersp[0],
        "users_scales": usersp[1],
        "shelves_words": shelvesp[0],
        "shelves_scales": shelvesp[1],
        "offs": striped8(idx),
        "offs2": striped8(idx2),
        "offs3": striped8(idx3),
        "offs4": striped8(idx4),
        "offs5": striped8(idx5),
    }


def reference(query, keys_words, keys_scales, notes_words, notes_scales, users_words, users_scales, shelves_words, shelves_scales, offs, offs2, offs3, offs4, offs5):
    idx = unstriped8(offs)
    idx2 = unstriped8(offs2)
    idx3 = unstriped8(offs3)
    idx4 = unstriped8(offs4)
    idx5 = unstriped8(offs5)
    keysu = unpack_weight(keys_words, keys_scales, "e2m1")
    notesu = unpack_weight(notes_words, notes_scales, "e4m3")
    usersu = unpack_weight(users_words, users_scales, "e2m1")
    shelvesu = unpack_weight(shelves_words, shelves_scales, "e4m3")
    queryq = mxq(f64(query), 0, "e4m3")
    a = queryq.T @ keysu
    b = queryq.T @ notesu
    c0 = queryq.T @ usersu
    d0 = queryq.T @ shelvesu
    w = np.maximum(pick8(a, idx, 16), pick8(d0, idx4, 16))
    r = np.minimum(w, pick8(b, idx2, 16))
    v = r - pick8(c0, idx3, 16)
    f1 = np.zeros((Q, X))
    f1[np.arange(Q)[:, None], idx3[np.arange(Q) % 128 // 16]] = v
    cc = c0 + f1
    y = pick8(cc, idx5, 16) + w
    return y

@@ -1,0 +1,126 @@
+from contextlib import ExitStack
+
+import concourse.mybir as mybir
+
+F32 = mybir.dt.float32
+BF16 = mybir.dt.bfloat16
+I32 = mybir.dt.int32
+U32 = mybir.dt.uint32
+U16 = mybir.dt.uint16
+U8 = mybir.dt.uint8
+FP8X4 = mybir.dt.float8_e4m3fn_x4
+FP4X4 = mybir.dt.float4_e2m1fn_x4
+ALU = mybir.AluOpType
+COPY = mybir.ActivationFunctionType.Copy
+
+P = 128
+D = 512
+COLS = 1024
+SLOTS = 512
+BANK = 512
+HALF = SLOTS // 2
+FLOPS = 2 * P * D * COLS * 4
+
+
+def tile_attend_substitutes_four_kernel(tc, query, keys_words, keys_scales, notes_words, notes_scales,
+                                         users_words, users_scales, shelves_words, shelves_scales,
+                                         offs, offs2, offs3, offs4, offs5, out):
+    nc = tc.nc
+    with ExitStack() as ctx:
+        lists = ctx.enter_context(tc.tile_pool(name="lists", bufs=1))
+        sb = ctx.enter_context(tc.tile_pool(name="sb", bufs=1))
+        psum = ctx.enter_context(tc.psum_pool(name="psum", bufs=1))
+
+        def load_words(name, words, fp4):
+            width = COLS * (2 if fp4 else 4)
+            t = sb.tile([P, width], U8, name=name + "_w", align_bytes=64)
+            src = words[0] if fp4 else words[0].rearrange("p n t -> p (n t)")
+            nc.sync.dma_start(out=t[:].bitcast(I32), in_=src.bitcast(I32))
+            return t
+
+        def load_scales(name, scales, queues):
+            t = sb.tile([P, COLS], U8, name=name + "_s", align_bytes=64)
+            for quad in range(4):
+                queues[quad].dma_start(out=t[32 * quad:32 * quad + 4, :].bitcast(I32),
+                                       in_=scales[0, 4 * quad:4 * quad + 4, :].bitcast(I32))
+            return t
+
+        def load_list(name, src):
+            t = lists.tile([P, SLOTS // 16], U16, name=name)
+            nc.sync.dma_start(t[:], src)
+            return t
+
+        q_raw = sb.tile([P, 4, P], F32, name="q_raw")
+        nc.sync.dma_start(out=q_raw[:], in_=query.rearrange("(p j) w -> p j w", j=4))
+        keys_w = load_words("keys", keys_words, True)
+        keys_s = load_scales("keys", keys_scales, [nc.scalar] * 4)
+        shelves_w = load_words("shelves", shelves_words, False)
+        shelves_s = load_scales("shelves", shelves_scales, [nc.scalar] * 4)
+        users_s = load_scales("users", users_scales, [nc.gpsimd] * 4)
+        l_a = load_list("l_a", offs)
+        l_d = load_list("l_d", offs4)
+        notes_w = load_words("notes", notes_words, False)
+        notes_s = load_scales("notes", notes_scales, [nc.sync] * 4)
+        users_w = load_words("users", users_words, True)
+        l_b = load_list("l_b", offs2)
+        l_c = load_list("l_c", offs3)
+        l_y = load_list("l_y", offs5)
+
+        f1 = sb.tile([P, COLS], F32, name="f1")
+        nc.vector.memset(f1[:], 0.0)
+
+        q_bf = sb.tile([P, P, 4], BF16, name="q_bf", align_bytes=64)
+        nc.vector.tensor_copy(out=q_bf[:].rearrange("p (c i) t -> p c t i", i=4),
+                              in_=q_raw[:].rearrange("p t (c i) -> p c t i", i=4))
+        q_codes = sb.tile([P, P], U32, name="q_codes", align_bytes=64)
+        q_scale = sb.tile([P, P], U8, name="q_scale", align_bytes=64)
+        nc.vector.quantize_mx(out=q_codes[:].bitcast(FP8X4), scales=q_scale[:],
+                              in_=q_bf[:].rearrange("p c t -> p (c t)"))
+
+        def scores(name, words, scales, fp4):
+            whole = sb.tile([P, COLS], F32, name=name)
+            per_col = 2 if fp4 else 4
+            banks = []
+            for h in range(2):
+                bank = psum.tile([P, BANK], F32, name=name + "_bank%d" % h)
+                moving = words[:, h * BANK * per_col:(h + 1) * BANK * per_col]
+                nc.tensor.matmul_mx(out=bank[:], lhsT=q_codes[:].bitcast(FP8X4), lhsT_scale=q_scale[:],
+                                    rhs=moving.bitcast(FP4X4 if fp4 else FP8X4),
+                                    rhs_scale=scales[:, h * BANK:(h + 1) * BANK], start=True, stop=True)
+                banks.append(bank)
+            nc.scalar.copy(out=whole[:, :BANK], in_=banks[0][:])
+            nc.vector.tensor_copy(out=whole[:, BANK:], in_=banks[1][:])
+            return whole
+
+        def half(lst, h):
+            return lst[:, h * HALF // 16:(h + 1) * HALF // 16]
+
+        def halves(name):
+            return [sb.tile([P, HALF], F32, name=name + "%d" % h) for h in range(2)]
+
+        ga, gd, gb, neg_gc, w, r, y = (halves(n) for n in ("ga", "gd", "gb", "neg_gc", "w", "r", "y"))
+
+        a = scores("a", keys_w, keys_s, True)
+        nc.vector.tensor_copy(ga[0][:], a[:].indirect(half(l_a, 0)))
+        nc.scalar.activation(ga[1][:], a[:].indirect(half(l_a, 1)), COPY)
+        d0 = scores("d0", shelves_w, shelves_s, False)
+        nc.vector.tensor_copy(gd[0][:], d0[:].indirect(half(l_d, 0)))
+        nc.scalar.activation(gd[1][:], d0[:].indirect(half(l_d, 1)), COPY)
+        nc.vector.tensor_tensor(w[0][:], ga[0][:], gd[0][:], ALU.max)
+        b = scores("b", notes_w, notes_s, False)
+        nc.scalar.activation(gb[0][:], b[:].indirect(half(l_b, 0)), COPY)
+        nc.vector.tensor_tensor(w[1][:], ga[1][:], gd[1][:], ALU.max)
+        c0 = scores("c0", users_w, users_s, True)
+        nc.vector.tensor_tensor(r[0][:], w[0][:], gb[0][:], ALU.min)
+        nc.scalar.activation(neg_gc[0][:], c0[:].indirect(half(l_c, 0)), COPY, scale=-1.0)
+        nc.scalar.activation(gb[1][:], b[:].indirect(half(l_b, 1)), COPY)
+        nc.scalar.activation(neg_gc[1][:], c0[:].indirect(half(l_c, 1)), COPY, scale=-1.0)
+        nc.vector.tensor_tensor(f1[:].indirect(half(l_c, 0)), r[0][:], neg_gc[0][:], ALU.add)
+        nc.vector.tensor_tensor(r[1][:], w[1][:], gb[1][:], ALU.min)
+        nc.vector.tensor_tensor(f1[:].indirect(half(l_c, 1)), r[1][:], neg_gc[1][:], ALU.add)
+
+        cc = sb.tile([P, COLS], F32, name="cc")
+        nc.vector.tensor_tensor(cc[:], c0[:], f1[:], ALU.add)
+        for h, queue in enumerate((nc.scalar, nc.sync)):
+            nc.vector.tensor_tensor(y[h][:], cc[:].indirect(half(l_y, h)), w[h][:], ALU.add)
+            queue.dma_start(out=out[:, h * HALF:(h + 1) * HALF], in_=y[h][:])

@@ -38,12 +38,9 @@ def tile_attend_substitutes_four_kernel(tc, query, keys_words, keys_scales, note
             nc.sync.dma_start(out=t[:].bitcast(I32), in_=src.bitcast(I32))
             return t
 
-        def load_scales(name, scales, queues):
-            t = sb.tile([P, COLS], U8, name=name + "_s", align_bytes=64)
-            for quad in range(4):
-                queues[quad].dma_start(out=t[32 * quad:32 * quad + 4, :].bitcast(I32),
-                                       in_=scales[0, 4 * quad:4 * quad + 4, :].bitcast(I32))
-            return t
+        def load_scales(t, scales, quad, queue):
+            queue.dma_start(out=t[32 * quad:32 * quad + 4, :].bitcast(I32),
+                            in_=scales[0, 4 * quad:4 * quad + 4, :].bitcast(I32))
 
         def load_list(name, src):
             t = lists.tile([P, SLOTS // 16], U16, name=name)
@@ -52,16 +49,26 @@ def tile_attend_substitutes_four_kernel(tc, query, keys_words, keys_scales, note
 
         q_raw = sb.tile([P, 4, P], F32, name="q_raw")
         nc.sync.dma_start(out=q_raw[:], in_=query.rearrange("(p j) w -> p j w", j=4))
+        keys_s, shelves_s, notes_s, users_s = (
+            sb.tile([P, COLS], U8, name=n + "_s", align_bytes=64) for n in ("keys", "shelves", "notes", "users"))
+        for quad in range(4):
+            load_scales(keys_s, keys_scales, quad, nc.scalar)
+        for quad in (2, 3):
+            load_scales(notes_s, notes_scales, quad, nc.gpsimd)
+        for quad in (0, 1):
+            load_scales(users_s, users_scales, quad, nc.gpsimd)
         keys_w = load_words("keys", keys_words, True)
-        keys_s = load_scales("keys", keys_scales, [nc.scalar] * 4)
         shelves_w = load_words("shelves", shelves_words, False)
-        shelves_s = load_scales("shelves", shelves_scales, [nc.scalar] * 4)
-        users_s = load_scales("users", users_scales, [nc.gpsimd] * 4)
         l_a = load_list("l_a", offs)
-        l_d = load_list("l_d", offs4)
+        for quad in range(4):
+            load_scales(shelves_s, shelves_scales, quad, nc.sync)
         notes_w = load_words("notes", notes_words, False)
-        notes_s = load_scales("notes", notes_scales, [nc.sync] * 4)
+        l_d = load_list("l_d", offs4)
+        for quad in (0, 1):
+            load_scales(notes_s, notes_scales, quad, nc.sync)
         users_w = load_words("users", users_words, True)
+        for quad in (2, 3):
+            load_scales(users_s, users_scales, quad, nc.sync)
         l_b = load_list("l_b", offs2)
         l_c = load_list("l_c", offs3)
         l_y = load_list("l_y", offs5)
@@ -77,7 +84,7 @@ def tile_attend_substitutes_four_kernel(tc, query, keys_words, keys_scales, note
         nc.vector.quantize_mx(out=q_codes[:].bitcast(FP8X4), scales=q_scale[:],
                               in_=q_bf[:].rearrange("p c t -> p (c t)"))
 
-        def scores(name, words, scales, fp4):
+        def scores(name, words, scales, fp4, second_copy):
             whole = sb.tile([P, COLS], F32, name=name)
             per_col = 2 if fp4 else 4
             banks = []
@@ -89,7 +96,7 @@ def tile_attend_substitutes_four_kernel(tc, query, keys_words, keys_scales, note
                                     rhs_scale=scales[:, h * BANK:(h + 1) * BANK], start=True, stop=True)
                 banks.append(bank)
             nc.scalar.copy(out=whole[:, :BANK], in_=banks[0][:])
-            nc.vector.tensor_copy(out=whole[:, BANK:], in_=banks[1][:])
+            second_copy(out=whole[:, BANK:], in_=banks[1][:])
             return whole
 
         def half(lst, h):
@@ -100,27 +107,30 @@ def tile_attend_substitutes_four_kernel(tc, query, keys_words, keys_scales, note
 
         ga, gd, gb, neg_gc, w, r, y = (halves(n) for n in ("ga", "gd", "gb", "neg_gc", "w", "r", "y"))
 
-        a = scores("a", keys_w, keys_s, True)
+        a = scores("a", keys_w, keys_s, True, nc.vector.tensor_copy)
+        d0 = scores("d0", shelves_w, shelves_s, False, nc.scalar.copy)
+        b = scores("b", notes_w, notes_s, False, nc.scalar.copy)
+        c0 = scores("c0", users_w, users_s, True, nc.vector.tensor_copy)
         nc.vector.tensor_copy(ga[0][:], a[:].indirect(half(l_a, 0)))
-        nc.scalar.activation(ga[1][:], a[:].indirect(half(l_a, 1)), COPY)
-        d0 = scores("d0", shelves_w, shelves_s, False)
+        nc.vector.tensor_copy(ga[1][:], a[:].indirect(half(l_a, 1)))
         nc.vector.tensor_copy(gd[0][:], d0[:].indirect(half(l_d, 0)))
-        nc.scalar.activation(gd[1][:], d0[:].indirect(half(l_d, 1)), COPY)
         nc.vector.tensor_tensor(w[0][:], ga[0][:], gd[0][:], ALU.max)
-        b = scores("b", notes_w, notes_s, False)
-        nc.scalar.activation(gb[0][:], b[:].indirect(half(l_b, 0)), COPY)
-        nc.vector.tensor_tensor(w[1][:], ga[1][:], gd[1][:], ALU.max)
-        c0 = scores("c0", users_w, users_s, True)
+        nc.vector.tensor_copy(gb[0][:], b[:].indirect(half(l_b, 0)))
         nc.vector.tensor_tensor(r[0][:], w[0][:], gb[0][:], ALU.min)
-        nc.scalar.activation(neg_gc[0][:], c0[:].indirect(half(l_c, 0)), COPY, scale=-1.0)
+        nc.vector.tensor_scalar(neg_gc[0][:], c0[:].indirect(half(l_c, 0)), -1.0, 0.0, ALU.mult, ALU.add)
+        nc.scalar.activation(gd[1][:], d0[:].indirect(half(l_d, 1)), COPY)
         nc.scalar.activation(gb[1][:], b[:].indirect(half(l_b, 1)), COPY)
         nc.scalar.activation(neg_gc[1][:], c0[:].indirect(half(l_c, 1)), COPY, scale=-1.0)
         nc.vector.tensor_tensor(f1[:].indirect(half(l_c, 0)), r[0][:], neg_gc[0][:], ALU.add)
+        nc.vector.tensor_tensor(w[1][:], ga[1][:], gd[1][:], ALU.max)
         nc.vector.tensor_tensor(r[1][:], w[1][:], gb[1][:], ALU.min)
         nc.vector.tensor_tensor(f1[:].indirect(half(l_c, 1)), r[1][:], neg_gc[1][:], ALU.add)
 
         cc = sb.tile([P, COLS], F32, name="cc")
         nc.vector.tensor_tensor(cc[:], c0[:], f1[:], ALU.add)
-        for h, queue in enumerate((nc.scalar, nc.sync)):
-            nc.vector.tensor_tensor(y[h][:], cc[:].indirect(half(l_y, h)), w[h][:], ALU.add)
+        g_cc = sb.tile([P, HALF], F32, name="g_cc")
+        nc.scalar.activation(g_cc[:], cc[:].indirect(half(l_y, 1)), COPY)
+        nc.vector.tensor_tensor(y[0][:], cc[:].indirect(half(l_y, 0)), w[0][:], ALU.add)
+        nc.vector.tensor_tensor(y[1][:], g_cc[:], w[1][:], ALU.add)
+        for h, queue in enumerate((nc.sync, nc.scalar)):
             queue.dma_start(out=out[:, h * HALF:(h + 1) * HALF], in_=y[h][:])

@@ -48,28 +48,29 @@ def tile_attend_substitutes_four_kernel(tc, query, keys_words, keys_scales, note
             return t
 
         q_raw = sb.tile([P, 4, P], F32, name="q_raw")
-        nc.sync.dma_start(out=q_raw[:], in_=query.rearrange("(p j) w -> p j w", j=4))
+        nc.scalar.dma_start(out=q_raw[:], in_=query.rearrange("(p j) w -> p j w", j=4))
         keys_s, shelves_s, notes_s, users_s = (
             sb.tile([P, COLS], U8, name=n + "_s", align_bytes=64) for n in ("keys", "shelves", "notes", "users"))
         for quad in range(4):
-            load_scales(keys_s, keys_scales, quad, nc.scalar)
+            load_scales(keys_s, keys_scales, quad, nc.scalar if quad < 2 else nc.sync)
+        load_scales(shelves_s, shelves_scales, 3, nc.gpsimd)
         for quad in (2, 3):
             load_scales(notes_s, notes_scales, quad, nc.gpsimd)
-        for quad in (0, 1):
-            load_scales(users_s, users_scales, quad, nc.gpsimd)
+        load_scales(users_s, users_scales, 0, nc.gpsimd)
+        load_scales(shelves_s, shelves_scales, 0, nc.sync)
         keys_w = load_words("keys", keys_words, True)
         shelves_w = load_words("shelves", shelves_words, False)
-        l_a = load_list("l_a", offs)
-        for quad in range(4):
+        for quad in (1, 2):
             load_scales(shelves_s, shelves_scales, quad, nc.sync)
-        notes_w = load_words("notes", notes_words, False)
+        l_a = load_list("l_a", offs)
         l_d = load_list("l_d", offs4)
+        notes_w = load_words("notes", notes_words, False)
         for quad in (0, 1):
             load_scales(notes_s, notes_scales, quad, nc.sync)
         users_w = load_words("users", users_words, True)
-        for quad in (2, 3):
-            load_scales(users_s, users_scales, quad, nc.sync)
         l_b = load_list("l_b", offs2)
+        for quad in (1, 2, 3):
+            load_scales(users_s, users_scales, quad, nc.sync)
         l_c = load_list("l_c", offs3)
         l_y = load_list("l_y", offs5)
 
@@ -84,19 +85,17 @@ def tile_attend_substitutes_four_kernel(tc, query, keys_words, keys_scales, note
         nc.vector.quantize_mx(out=q_codes[:].bitcast(FP8X4), scales=q_scale[:],
                               in_=q_bf[:].rearrange("p c t -> p (c t)"))
 
-        def scores(name, words, scales, fp4, second_copy):
+        def scores(name, words, scales, fp4, first_bank, copies):
             whole = sb.tile([P, COLS], F32, name=name)
             per_col = 2 if fp4 else 4
-            banks = []
-            for h in range(2):
-                bank = psum.tile([P, BANK], F32, name=name + "_bank%d" % h)
-                moving = words[:, h * BANK * per_col:(h + 1) * BANK * per_col]
+            n = COLS // len(copies)
+            for h, copy in enumerate(copies):
+                bank = psum.tile([P, n], F32, name="bank%d" % (first_bank + h))
+                moving = words[:, h * n * per_col:(h + 1) * n * per_col]
                 nc.tensor.matmul_mx(out=bank[:], lhsT=q_codes[:].bitcast(FP8X4), lhsT_scale=q_scale[:],
                                     rhs=moving.bitcast(FP4X4 if fp4 else FP8X4),
-                                    rhs_scale=scales[:, h * BANK:(h + 1) * BANK], start=True, stop=True)
-                banks.append(bank)
-            nc.scalar.copy(out=whole[:, :BANK], in_=banks[0][:])
-            second_copy(out=whole[:, BANK:], in_=banks[1][:])
+                                    rhs_scale=scales[:, h * n:(h + 1) * n], start=True, stop=True)
+                copy(out=whole[:, h * n:(h + 1) * n], in_=bank[:])
             return whole
 
         def half(lst, h):
@@ -105,32 +104,34 @@ def tile_attend_substitutes_four_kernel(tc, query, keys_words, keys_scales, note
         def halves(name):
             return [sb.tile([P, HALF], F32, name=name + "%d" % h) for h in range(2)]
 
-        ga, gd, gb, neg_gc, w, r, y = (halves(n) for n in ("ga", "gd", "gb", "neg_gc", "w", "r", "y"))
+        ga, gd, gb, w, r = (sb.tile([P, SLOTS], F32, name=n) for n in ("ga", "gd", "gb", "w", "r"))
+        neg_gc, y = halves("neg_gc"), halves("y")
+        cols = [slice(0, HALF), slice(HALF, SLOTS)]
 
-        a = scores("a", keys_w, keys_s, True, nc.vector.tensor_copy)
-        d0 = scores("d0", shelves_w, shelves_s, False, nc.scalar.copy)
-        b = scores("b", notes_w, notes_s, False, nc.scalar.copy)
-        c0 = scores("c0", users_w, users_s, True, nc.vector.tensor_copy)
-        nc.vector.tensor_copy(ga[0][:], a[:].indirect(half(l_a, 0)))
-        nc.vector.tensor_copy(ga[1][:], a[:].indirect(half(l_a, 1)))
-        nc.vector.tensor_copy(gd[0][:], d0[:].indirect(half(l_d, 0)))
-        nc.vector.tensor_tensor(w[0][:], ga[0][:], gd[0][:], ALU.max)
-        nc.vector.tensor_copy(gb[0][:], b[:].indirect(half(l_b, 0)))
-        nc.vector.tensor_tensor(r[0][:], w[0][:], gb[0][:], ALU.min)
-        nc.vector.tensor_scalar(neg_gc[0][:], c0[:].indirect(half(l_c, 0)), -1.0, 0.0, ALU.mult, ALU.add)
-        nc.scalar.activation(gd[1][:], d0[:].indirect(half(l_d, 1)), COPY)
-        nc.scalar.activation(gb[1][:], b[:].indirect(half(l_b, 1)), COPY)
-        nc.scalar.activation(neg_gc[1][:], c0[:].indirect(half(l_c, 1)), COPY, scale=-1.0)
-        nc.vector.tensor_tensor(f1[:].indirect(half(l_c, 0)), r[0][:], neg_gc[0][:], ALU.add)
-        nc.vector.tensor_tensor(w[1][:], ga[1][:], gd[1][:], ALU.max)
-        nc.vector.tensor_tensor(r[1][:], w[1][:], gb[1][:], ALU.min)
-        nc.vector.tensor_tensor(f1[:].indirect(half(l_c, 1)), r[1][:], neg_gc[1][:], ALU.add)
+        on_s, on_v = nc.scalar.copy, nc.vector.tensor_copy
+        a = scores("a", keys_w, keys_s, True, 0, (on_s, on_v, on_s, on_v))
+        nc.vector.tensor_copy(ga[:, cols[0]], a[:].indirect(half(l_a, 0)))
+        nc.scalar.activation(ga[:, cols[1]], a[:].indirect(half(l_a, 1)), COPY)
+        d0 = scores("d0", shelves_w, shelves_s, False, 4, (on_s, on_v))
+        for h in range(2):
+            nc.vector.tensor_copy(gd[:, cols[h]], d0[:].indirect(half(l_d, h)))
+        b = scores("b", notes_w, notes_s, False, 6, (on_s, on_s))
+        for h in range(2):
+            nc.vector.tensor_tensor(w[:, cols[h]], ga[:, cols[h]], gd[:, cols[h]], ALU.max)
+        for h in range(2):
+            nc.vector.tensor_copy(gb[:, cols[h]], b[:].indirect(half(l_b, h)))
+        c0 = scores("c0", users_w, users_s, True, 0, (on_s, on_s))
+        for h in range(2):
+            nc.vector.tensor_tensor(r[:, cols[h]], w[:, cols[h]], gb[:, cols[h]], ALU.min)
+        for h in range(2):
+            nc.scalar.activation(neg_gc[h][:], c0[:].indirect(half(l_c, h)), COPY, scale=-1.0)
+            nc.vector.tensor_tensor(f1[:].indirect(half(l_c, h)), r[:, cols[h]], neg_gc[h][:], ALU.add)
 
         cc = sb.tile([P, COLS], F32, name="cc")
         nc.vector.tensor_tensor(cc[:], c0[:], f1[:], ALU.add)
         g_cc = sb.tile([P, HALF], F32, name="g_cc")
         nc.scalar.activation(g_cc[:], cc[:].indirect(half(l_y, 1)), COPY)
-        nc.vector.tensor_tensor(y[0][:], cc[:].indirect(half(l_y, 0)), w[0][:], ALU.add)
-        nc.vector.tensor_tensor(y[1][:], g_cc[:], w[1][:], ALU.add)
+        nc.vector.tensor_tensor(y[0][:], cc[:].indirect(half(l_y, 0)), w[:, cols[0]], ALU.add)
+        nc.vector.tensor_tensor(y[1][:], g_cc[:], w[:, cols[1]], ALU.add)
         for h, queue in enumerate((nc.sync, nc.scalar)):
             queue.dma_start(out=out[:, h * HALF:(h + 1) * HALF], in_=y[h][:])

@@ -75,7 +75,8 @@ def tile_attend_substitutes_four_kernel(tc, query, keys_words, keys_scales, note
         l_y = load_list("l_y", offs5)
 
         f1 = sb.tile([P, COLS], F32, name="f1")
-        nc.vector.memset(f1[:], 0.0)
+        nc.vector.memset(f1[:, :BANK + 1], 0.0)
+        nc.vector.memset(f1[:, BANK + 1:], 0.0)
 
         q_bf = sb.tile([P, P, 4], BF16, name="q_bf", align_bytes=64)
         nc.vector.tensor_copy(out=q_bf[:].rearrange("p (c i) t -> p c t i", i=4),
@@ -109,10 +110,10 @@ def tile_attend_substitutes_four_kernel(tc, query, keys_words, keys_scales, note
         cols = [slice(0, HALF), slice(HALF, SLOTS)]
 
         on_s, on_v = nc.scalar.copy, nc.vector.tensor_copy
-        a = scores("a", keys_w, keys_s, True, 0, (on_s, on_v, on_s, on_v))
+        a = scores("a", keys_w, keys_s, True, 0, (on_s, on_v))
         nc.vector.tensor_copy(ga[:, cols[0]], a[:].indirect(half(l_a, 0)))
         nc.scalar.activation(ga[:, cols[1]], a[:].indirect(half(l_a, 1)), COPY)
-        d0 = scores("d0", shelves_w, shelves_s, False, 4, (on_s, on_v))
+        d0 = scores("d0", shelves_w, shelves_s, False, 2, (on_s, on_v, on_s, on_v))
         for h in range(2):
             nc.vector.tensor_copy(gd[:, cols[h]], d0[:].indirect(half(l_d, h)))
         b = scores("b", notes_w, notes_s, False, 6, (on_s, on_s))

@@ -15,10 +15,15 @@ COPY = mybir.ActivationFunctionType.Copy
 
 P = 128
 D = 512
+PACK = 4
+QUADRANT = 32
+SCALE_ROWS = 4
 COLS = 1024
 SLOTS = 512
-BANK = 512
+HEAD = 16
 HALF = SLOTS // 2
+BANK = 512
+SPLIT = 800
 FLOPS = 2 * P * D * COLS * 4
 
 
@@ -39,20 +44,22 @@ def tile_attend_substitutes_four_kernel(tc, query, keys_words, keys_scales, note
             return t
 
         def load_scales(t, scales, quad, queue):
-            queue.dma_start(out=t[32 * quad:32 * quad + 4, :].bitcast(I32),
-                            in_=scales[0, 4 * quad:4 * quad + 4, :].bitcast(I32))
+            queue.dma_start(out=t[QUADRANT * quad:QUADRANT * quad + SCALE_ROWS, :].bitcast(I32),
+                            in_=scales[0, SCALE_ROWS * quad:SCALE_ROWS * (quad + 1), :].bitcast(I32))
 
         def load_list(name, src):
-            t = lists.tile([P, SLOTS // 16], U16, name=name)
+            t = lists.tile([P, SLOTS // HEAD], U16, name=name)
             nc.sync.dma_start(t[:], src)
             return t
 
-        q_raw = sb.tile([P, 4, P], F32, name="q_raw")
-        nc.scalar.dma_start(out=q_raw[:], in_=query.rearrange("(p j) w -> p j w", j=4))
+        q_raw = sb.tile([P, PACK, P], F32, name="q_raw")
+        nc.scalar.dma_start(out=q_raw[:], in_=query.rearrange("(p j) w -> p j w", j=PACK))
         keys_s, shelves_s, notes_s, users_s = (
             sb.tile([P, COLS], U8, name=n + "_s", align_bytes=64) for n in ("keys", "shelves", "notes", "users"))
-        for quad in range(4):
-            load_scales(keys_s, keys_scales, quad, nc.scalar if quad < 2 else nc.sync)
+        for quad in (0, 1):
+            load_scales(keys_s, keys_scales, quad, nc.scalar)
+        for quad in (2, 3):
+            load_scales(keys_s, keys_scales, quad, nc.sync)
         load_scales(shelves_s, shelves_scales, 3, nc.gpsimd)
         for quad in (2, 3):
             load_scales(notes_s, notes_scales, quad, nc.gpsimd)
@@ -62,23 +69,22 @@ def tile_attend_substitutes_four_kernel(tc, query, keys_words, keys_scales, note
         shelves_w = load_words("shelves", shelves_words, False)
         for quad in (1, 2):
             load_scales(shelves_s, shelves_scales, quad, nc.sync)
-        l_a = load_list("l_a", offs)
-        l_d = load_list("l_d", offs4)
         notes_w = load_words("notes", notes_words, False)
+        list_a = load_list("list_a", offs)
+        list_d = load_list("list_d", offs4)
         for quad in (0, 1):
             load_scales(notes_s, notes_scales, quad, nc.sync)
+        list_b = load_list("list_b", offs2)
         users_w = load_words("users", users_words, True)
-        l_b = load_list("l_b", offs2)
         for quad in (1, 2, 3):
             load_scales(users_s, users_scales, quad, nc.sync)
-        l_c = load_list("l_c", offs3)
-        l_y = load_list("l_y", offs5)
+        list_c = load_list("list_c", offs3)
+        list_cc = load_list("list_cc", offs5)
 
         f1 = sb.tile([P, COLS], F32, name="f1")
-        nc.vector.memset(f1[:, :BANK + 1], 0.0)
-        nc.vector.memset(f1[:, BANK + 1:], 0.0)
+        nc.vector.memset(f1[:], 0.0)
 
-        q_bf = sb.tile([P, P, 4], BF16, name="q_bf", align_bytes=64)
+        q_bf = sb.tile([P, P, PACK], BF16, name="q_bf", align_bytes=64)
         nc.vector.tensor_copy(out=q_bf[:].rearrange("p (c i) t -> p c t i", i=4),
                               in_=q_raw[:].rearrange("p t (c i) -> p c t i", i=4))
         q_codes = sb.tile([P, P], U32, name="q_codes", align_bytes=64)
@@ -90,49 +96,55 @@ def tile_attend_substitutes_four_kernel(tc, query, keys_words, keys_scales, note
             whole = sb.tile([P, COLS], F32, name=name)
             per_col = 2 if fp4 else 4
             n = COLS // len(copies)
-            for h, copy in enumerate(copies):
-                bank = psum.tile([P, n], F32, name="bank%d" % (first_bank + h))
-                moving = words[:, h * n * per_col:(h + 1) * n * per_col]
+            banks = []
+            for j, copy in enumerate(copies):
+                bank = psum.tile([P, n], F32, name="bank%d" % (first_bank + j))
+                moving = words[:, j * n * per_col:(j + 1) * n * per_col]
                 nc.tensor.matmul_mx(out=bank[:], lhsT=q_codes[:].bitcast(FP8X4), lhsT_scale=q_scale[:],
                                     rhs=moving.bitcast(FP4X4 if fp4 else FP8X4),
-                                    rhs_scale=scales[:, h * n:(h + 1) * n], start=True, stop=True)
-                copy(out=whole[:, h * n:(h + 1) * n], in_=bank[:])
-            return whole
+                                    rhs_scale=scales[:, j * n:(j + 1) * n], start=True, stop=True)
+                copy(out=whole[:, j * n:(j + 1) * n], in_=bank[:])
+                banks.append(bank)
+            return whole, banks
 
-        def half(lst, h):
-            return lst[:, h * HALF // 16:(h + 1) * HALF // 16]
+        def half(list_tile, h):
+            return list_tile[:, h * HALF // HEAD:(h + 1) * HALF // HEAD]
 
         def halves(name):
             return [sb.tile([P, HALF], F32, name=name + "%d" % h) for h in range(2)]
 
         ga, gd, gb, w, r = (sb.tile([P, SLOTS], F32, name=n) for n in ("ga", "gd", "gb", "w", "r"))
         neg_gc, y = halves("neg_gc"), halves("y")
-        cols = [slice(0, HALF), slice(HALF, SLOTS)]
+        slots = [slice(0, HALF), slice(HALF, SLOTS)]
 
-        on_s, on_v = nc.scalar.copy, nc.vector.tensor_copy
-        a = scores("a", keys_w, keys_s, True, 0, (on_s, on_v))
-        nc.vector.tensor_copy(ga[:, cols[0]], a[:].indirect(half(l_a, 0)))
-        nc.scalar.activation(ga[:, cols[1]], a[:].indirect(half(l_a, 1)), COPY)
-        d0 = scores("d0", shelves_w, shelves_s, False, 2, (on_s, on_v, on_s, on_v))
+        on_scalar, on_vector = nc.scalar.copy, nc.vector.tensor_copy
+        a = scores("a", keys_w, keys_s, True, 0, (on_scalar, on_vector))[0]
+        nc.vector.tensor_copy(ga[:, slots[0]], a[:].indirect(half(list_a, 0)))
+        nc.scalar.activation(ga[:, slots[1]], a[:].indirect(half(list_a, 1)), COPY)
+        d0 = scores("d0", shelves_w, shelves_s, False, 2, (on_scalar, on_vector) * 2)[0]
         for h in range(2):
-            nc.vector.tensor_copy(gd[:, cols[h]], d0[:].indirect(half(l_d, h)))
-        b = scores("b", notes_w, notes_s, False, 6, (on_s, on_s))
+            nc.vector.tensor_copy(gd[:, slots[h]], d0[:].indirect(half(list_d, h)))
+        b = scores("b", notes_w, notes_s, False, 6, (on_scalar, on_scalar))[0]
         for h in range(2):
-            nc.vector.tensor_tensor(w[:, cols[h]], ga[:, cols[h]], gd[:, cols[h]], ALU.max)
+            nc.vector.tensor_tensor(w[:, slots[h]], ga[:, slots[h]], gd[:, slots[h]], ALU.max)
         for h in range(2):
-            nc.vector.tensor_copy(gb[:, cols[h]], b[:].indirect(half(l_b, h)))
-        c0 = scores("c0", users_w, users_s, True, 0, (on_s, on_s))
+            nc.vector.tensor_copy(gb[:, slots[h]], b[:].indirect(half(list_b, h)))
+        c0, c0_banks = scores("c0", users_w, users_s, True, 0, (on_scalar, on_scalar))
         for h in range(2):
-            nc.vector.tensor_tensor(r[:, cols[h]], w[:, cols[h]], gb[:, cols[h]], ALU.min)
+            nc.vector.tensor_tensor(r[:, slots[h]], w[:, slots[h]], gb[:, slots[h]], ALU.min)
+
         for h in range(2):
-            nc.scalar.activation(neg_gc[h][:], c0[:].indirect(half(l_c, h)), COPY, scale=-1.0)
-            nc.vector.tensor_tensor(f1[:].indirect(half(l_c, h)), r[:, cols[h]], neg_gc[h][:], ALU.add)
+            nc.scalar.activation(neg_gc[h][:], c0[:].indirect(half(list_c, h)), COPY, scale=-1.0)
+            nc.vector.tensor_tensor(f1[:].indirect(half(list_c, h)), r[:, slots[h]], neg_gc[h][:], ALU.add)
 
         cc = sb.tile([P, COLS], F32, name="cc")
-        nc.vector.tensor_tensor(cc[:], c0[:], f1[:], ALU.add)
+        nc.gpsimd.tensor_tensor(cc[:, SPLIT:], f1[:, SPLIT:], c0[:, SPLIT:], ALU.add)
+        nc.vector.tensor_tensor(cc[:, :BANK], f1[:, :BANK], c0_banks[0][:], ALU.add)
+        nc.vector.tensor_tensor(cc[:, BANK:SPLIT], f1[:, BANK:SPLIT], c0_banks[1][:, :SPLIT - BANK], ALU.add)
+
         g_cc = sb.tile([P, HALF], F32, name="g_cc")
-        nc.scalar.activation(g_cc[:], cc[:].indirect(half(l_y, 1)), COPY)
-        nc.vector.tensor_tensor(y[0][:], cc[:].indirect(half(l_y, 0)), w[:, cols[0]], ALU.add)
-        nc.vector.tensor_tensor(y[1][:], g_cc[:], w[:, cols[1]], ALU.add)
+        nc.scalar.activation(g_cc[:], cc[:].indirect(half(list_cc, 1)), COPY)
+        nc.vector.tensor_tensor(y[0][:], cc[:].indirect(half(list_cc, 0)), w[:, slots[0]], ALU.add)
+        nc.vector.tensor_tensor(y[1][:], g_cc[:], w[:, slots[1]], ALU.add)
         for h, queue in enumerate((nc.sync, nc.scalar)):
-            queue.dma_start(out=out[:, h * HALF:(h + 1) * HALF], in_=y[h][:])
+            queue.dma_start(out=out[:, slots[h]], in_=y[h][:])

from contextlib import ExitStack

import concourse.mybir as mybir

F32 = mybir.dt.float32
BF16 = mybir.dt.bfloat16
I32 = mybir.dt.int32
U32 = mybir.dt.uint32
U16 = mybir.dt.uint16
U8 = mybir.dt.uint8
FP8X4 = mybir.dt.float8_e4m3fn_x4
FP4X4 = mybir.dt.float4_e2m1fn_x4
ALU = mybir.AluOpType
COPY = mybir.ActivationFunctionType.Copy

P = 128
D = 512
PACK = 4
QUADRANT = 32
SCALE_ROWS = 4
COLS = 1024
SLOTS = 512
HEAD = 16
HALF = SLOTS // 2
BANK = 512
SPLIT = 800
FLOPS = 2 * P * D * COLS * 4


def tile_attend_substitutes_four_kernel(tc, query, keys_words, keys_scales, notes_words, notes_scales,
                                         users_words, users_scales, shelves_words, shelves_scales,
                                         offs, offs2, offs3, offs4, offs5, out):
    nc = tc.nc
    with ExitStack() as ctx:
        lists = ctx.enter_context(tc.tile_pool(name="lists", bufs=1))
        sb = ctx.enter_context(tc.tile_pool(name="sb", bufs=1))
        psum = ctx.enter_context(tc.psum_pool(name="psum", bufs=1))

        def load_words(name, words, fp4):
            width = COLS * (2 if fp4 else 4)
            t = sb.tile([P, width], U8, name=name + "_w", align_bytes=64)
            src = words[0] if fp4 else words[0].rearrange("p n t -> p (n t)")
            nc.sync.dma_start(out=t[:].bitcast(I32), in_=src.bitcast(I32))
            return t

        def load_scales(t, scales, quad, queue):
            queue.dma_start(out=t[QUADRANT * quad:QUADRANT * quad + SCALE_ROWS, :].bitcast(I32),
                            in_=scales[0, SCALE_ROWS * quad:SCALE_ROWS * (quad + 1), :].bitcast(I32))

        def load_list(name, src):
            t = lists.tile([P, SLOTS // HEAD], U16, name=name)
            nc.sync.dma_start(t[:], src)
            return t

        q_raw = sb.tile([P, PACK, P], F32, name="q_raw")
        nc.scalar.dma_start(out=q_raw[:], in_=query.rearrange("(p j) w -> p j w", j=PACK))
        keys_s, shelves_s, notes_s, users_s = (
            sb.tile([P, COLS], U8, name=n + "_s", align_bytes=64) for n in ("keys", "shelves", "notes", "users"))
        for quad in (0, 1):
            load_scales(keys_s, keys_scales, quad, nc.scalar)
        for quad in (2, 3):
            load_scales(keys_s, keys_scales, quad, nc.sync)
        load_scales(shelves_s, shelves_scales, 3, nc.gpsimd)
        for quad in (2, 3):
            load_scales(notes_s, notes_scales, quad, nc.gpsimd)
        load_scales(users_s, users_scales, 0, nc.gpsimd)
        load_scales(shelves_s, shelves_scales, 0, nc.sync)
        keys_w = load_words("keys", keys_words, True)
        shelves_w = load_words("shelves", shelves_words, False)
        for quad in (1, 2):
            load_scales(shelves_s, shelves_scales, quad, nc.sync)
        notes_w = load_words("notes", notes_words, False)
        list_a = load_list("list_a", offs)
        list_d = load_list("list_d", offs4)
        for quad in (0, 1):
            load_scales(notes_s, notes_scales, quad, nc.sync)
        list_b = load_list("list_b", offs2)
        users_w = load_words("users", users_words, True)
        for quad in (1, 2, 3):
            load_scales(users_s, users_scales, quad, nc.sync)
        list_c = load_list("list_c", offs3)
        list_cc = load_list("list_cc", offs5)

        f1 = sb.tile([P, COLS], F32, name="f1")
        nc.vector.memset(f1[:], 0.0)

        q_bf = sb.tile([P, P, PACK], BF16, name="q_bf", align_bytes=64)
        nc.vector.tensor_copy(out=q_bf[:].rearrange("p (c i) t -> p c t i", i=4),
                              in_=q_raw[:].rearrange("p t (c i) -> p c t i", i=4))
        q_codes = sb.tile([P, P], U32, name="q_codes", align_bytes=64)
        q_scale = sb.tile([P, P], U8, name="q_scale", align_bytes=64)
        nc.vector.quantize_mx(out=q_codes[:].bitcast(FP8X4), scales=q_scale[:],
                              in_=q_bf[:].rearrange("p c t -> p (c t)"))

        def scores(name, words, scales, fp4, first_bank, copies):
            whole = sb.tile([P, COLS], F32, name=name)
            per_col = 2 if fp4 else 4
            n = COLS // len(copies)
            banks = []
            for j, copy in enumerate(copies):
                bank = psum.tile([P, n], F32, name="bank%d" % (first_bank + j))
                moving = words[:, j * n * per_col:(j + 1) * n * per_col]
                nc.tensor.matmul_mx(out=bank[:], lhsT=q_codes[:].bitcast(FP8X4), lhsT_scale=q_scale[:],
                                    rhs=moving.bitcast(FP4X4 if fp4 else FP8X4),
                                    rhs_scale=scales[:, j * n:(j + 1) * n], start=True, stop=True)
                copy(out=whole[:, j * n:(j + 1) * n], in_=bank[:])
                banks.append(bank)
            return whole, banks

        def half(list_tile, h):
            return list_tile[:, h * HALF // HEAD:(h + 1) * HALF // HEAD]

        def halves(name):
            return [sb.tile([P, HALF], F32, name=name + "%d" % h) for h in range(2)]

        ga, gd, gb, w, r = (sb.tile([P, SLOTS], F32, name=n) for n in ("ga", "gd", "gb", "w", "r"))
        neg_gc, y = halves("neg_gc"), halves("y")
        slots = [slice(0, HALF), slice(HALF, SLOTS)]

        on_scalar, on_vector = nc.scalar.copy, nc.vector.tensor_copy
        a = scores("a", keys_w, keys_s, True, 0, (on_scalar, on_vector))[0]
        nc.vector.tensor_copy(ga[:, slots[0]], a[:].indirect(half(list_a, 0)))
        nc.scalar.activation(ga[:, slots[1]], a[:].indirect(half(list_a, 1)), COPY)
        d0 = scores("d0", shelves_w, shelves_s, False, 2, (on_scalar, on_vector) * 2)[0]
        for h in range(2):
            nc.vector.tensor_copy(gd[:, slots[h]], d0[:].indirect(half(list_d, h)))
        b = scores("b", notes_w, notes_s, False, 6, (on_scalar, on_scalar))[0]
        for h in range(2):
            nc.vector.tensor_tensor(w[:, slots[h]], ga[:, slots[h]], gd[:, slots[h]], ALU.max)
        for h in range(2):
            nc.vector.tensor_copy(gb[:, slots[h]], b[:].indirect(half(list_b, h)))
        c0, c0_banks = scores("c0", users_w, users_s, True, 0, (on_scalar, on_scalar))
        for h in range(2):
            nc.vector.tensor_tensor(r[:, slots[h]], w[:, slots[h]], gb[:, slots[h]], ALU.min)

        for h in range(2):
            nc.scalar.activation(neg_gc[h][:], c0[:].indirect(half(list_c, h)), COPY, scale=-1.0)
            nc.vector.tensor_tensor(f1[:].indirect(half(list_c, h)), r[:, slots[h]], neg_gc[h][:], ALU.add)

        cc = sb.tile([P, COLS], F32, name="cc")
        nc.gpsimd.tensor_tensor(cc[:, SPLIT:], f1[:, SPLIT:], c0[:, SPLIT:], ALU.add)
        nc.vector.tensor_tensor(cc[:, :BANK], f1[:, :BANK], c0_banks[0][:], ALU.add)
        nc.vector.tensor_tensor(cc[:, BANK:SPLIT], f1[:, BANK:SPLIT], c0_banks[1][:, :SPLIT - BANK], ALU.add)

        g_cc = sb.tile([P, HALF], F32, name="g_cc")
        nc.scalar.activation(g_cc[:], cc[:].indirect(half(list_cc, 1)), COPY)
        nc.vector.tensor_tensor(y[0][:], cc[:].indirect(half(list_cc, 0)), w[:, slots[0]], ALU.add)
        nc.vector.tensor_tensor(y[1][:], g_cc[:], w[:, slots[1]], ALU.add)
        for h, queue in enumerate((nc.sync, nc.scalar)):
            queue.dma_start(out=out[:, slots[h]], in_=y[h][:])
